import numpy as np
import ml_dtypes


def mxq(x, axis, fmt="e4m3"):
    dtype, down = {"e4m3": (ml_dtypes.float8_e4m3fn, 7), "e5m2": (ml_dtypes.float8_e5m2, 14)}[fmt]
    v = np.moveaxis(np.asarray(x, np.float32).astype(ml_dtypes.bfloat16).astype(np.float64), axis, -1)
    blocks = v.reshape(v.shape[:-1] + (-1, 32))
    amax = np.abs(blocks).max(-1, keepdims=True)
    byte = np.maximum(np.where(amax > 0, np.frexp(amax)[1] - 1 + 127, 0) - down, 1)
    scale = np.exp2(byte - 127.0)
    codes = (blocks / scale).astype(np.float32).astype(dtype).astype(np.float64)
    return np.moveaxis((codes * scale).reshape(v.shape), -1, axis)


WIDE = False


def mx_kscale(k):
    if not WIDE:
        return np.ones(k)
    levels = np.array([10, -10, 5, -5, 0])
    if k % 512:
        return np.exp2(np.random.permutation(np.resize(levels, k // 32))).repeat(32)
    a = np.empty((k // 512, 16))
    for p in range(k // 512):
        a[p, :8] = np.random.permutation(np.resize(levels, 8))
        for g in range(8):
            far = levels[np.abs(levels - a[p, g]) >= 10]
            a[p, g + 8] = far[np.random.randint(len(far))]
    return np.exp2(a.ravel()).repeat(32)


def f64(x):
    return np.asarray(x).astype(np.float64)


def striped(idx):
    return np.tile(np.asarray(idx).reshape(-1, 16).T, (8, 1)).astype(np.uint16)


def unstriped(offs):
    return offs[:16].T.reshape(-1).astype(np.int64)


E2M1 = np.array([0.0, 0.5, 1.0, 1.5, 2.0, 3.0, 4.0, 6.0, -0.0, -0.5, -1.0, -1.5, -2.0, -3.0, -4.0, -6.0])


def pack_weight(w, fmt):
    k, n = w.shape
    w = f64(np.asarray(w, np.float32).astype(ml_dtypes.bfloat16)).reshape(k // 32, 32, n)
    amax = np.abs(w).max(1)
    if fmt == "e4m3":
        byte = np.frexp(amax)[1] - 1 + 127 - 7
    else:
        mant, ex = np.frexp(amax / 6.0)
        byte = np.where(mant > 0.5, ex, ex - 1) + 127
    byte = np.clip(np.where(amax > 0, byte, 1), 1, 254)
    scaled = (w * np.exp2(127.0 - byte)[:, None, :]).reshape(k, n).astype(np.float32)
    by_word = np.ascontiguousarray(scaled.reshape(k // 512, 128, 4, n).transpose(0, 1, 3, 2))
    if fmt == "e4m3":
        words = by_word.astype(ml_dtypes.float8_e4m3fn).view(np.uint8)
    else:
        c = by_word.astype(ml_dtypes.float4_e2m1fn).view(np.uint8) & 0xF
        words = (c[..., 0::2] | (c[..., 1::2] << 4)).reshape(k // 512, 128, 2 * n)
    return np.ascontiguousarray(words), np.ascontiguousarray(byte.astype(np.uint8).reshape(k // 512, 16, n))


def unpack_weight(words, scales, fmt):
    g, _, n = scales.shape
    words = np.ascontiguousarray(words).reshape(g, 128, n, -1)
    if fmt == "e4m3":
        vals = words.view(ml_dtypes.float8_e4m3fn).astype(np.float64)
    else:
        nib = np.empty((g, 128, n, 4), np.uint8)
        nib[..., 0::2] = words & 0xF
        nib[..., 1::2] = words >> 4
        vals = E2M1[nib]
    vals = vals * np.repeat(np.exp2(scales.astype(np.float64) - 127.0), 8, axis=1)[..., None]
    return vals.transpose(0, 1, 3, 2).reshape(g * 512, n)


def sigmoid(v):
    return 1.0 / (1.0 + np.exp(-v))


D, T, I, Q, E, Z, M = 512, 2048, 512, 256, 512, 1024, 1024


def setup_inputs():
    n = np.random.standard_normal
    idx = np.random.permutation(T)[:I]
    idx2 = np.random.permutation(Z)[:I]
    idx3 = np.random.permutation(Z)[:I]
    idx4 = np.random.permutation(M)[:Q]
    fd = mx_kscale(D)
    fi = mx_kscale(I)
    ti = np.ones(T)
    ti[idx] = fi
    keysp = pack_weight(n((D, T)) / fd[:, None], "e4m3")
    return {
        "query": (n((D, Q)) * 1.0 / np.sqrt(D) * fd[:, None]).astype(np.float32),
        "keys_words": keysp[0],
        "keys_scales": keysp[1],
        "os": (np.random.uniform(0.02, 0.08, (1, I)) * fi).astype(np.float32),
        "vals": (n((E, T)) / ti).astype(np.float32),
        "old": (n((E, M)) * 2.0).astype(np.float32),
        "fade": (np.random.uniform(0.3, 0.9, (1, M))).astype(np.float32),
        "offs": striped(idx),
        "offs2": striped(idx2),
        "offs3": striped(idx3),
        "offs4": striped(idx4),
    }


def reference(query, keys_words, keys_scales, os, vals, old, fade, offs, offs2, offs3, offs4):
    idx = unstriped(offs)
    idx2 = unstriped(offs2)
    idx3 = unstriped(offs3)
    idx4 = unstriped(offs4)
    keysu = unpack_weight(keys_words, keys_scales, "e4m3")
    queryq = mxq(f64(query), 0, "e4m3")
    keysidxg = keysu[:, idx]
    a = queryq.T @ keysidxg
    f0 = np.zeros((Q, Z))
    f0[:, idx2] = a
    s = a + f0[:, idx3]
    w = sigmoid(s)
    wo1 = w * f64(os)
    wt1 = wo1.T
    vt1 = f64(vals)[:, idx].T
    vt1q = mxq(vt1, 0, "e4m3")
    wt1q = mxq(wt1, 0, "e4m3")
    o = vt1q.T @ wt1q
    of = np.zeros((E, M))
    of[:, idx4] = o
    y = f64(old) * f64(fade) + of
    return y

@@ -1,0 +1,241 @@
+from contextlib import ExitStack
+
+import concourse.mybir as mybir
+from concourse.masks import make_identity
+
+D, T, I, Q, E, Z, M = 512, 2048, 512, 256, 512, 1024, 1024
+FLOPS = 2 * D * Q * I + 2 * I * E * Q
+
+F32 = mybir.dt.float32
+BF16 = mybir.dt.bfloat16
+I32 = mybir.dt.int32
+U32 = mybir.dt.uint32
+U16 = mybir.dt.uint16
+U8 = mybir.dt.uint8
+FP8X4 = mybir.dt.float8_e4m3fn_x4
+ADD = mybir.AluOpType.add
+MULT = mybir.AluOpType.mult
+COPY = mybir.ActivationFunctionType.Copy
+SIGMOID = mybir.ActivationFunctionType.Sigmoid
+
+P = 128
+PACK = 4
+BANK = 512
+Q_TILES = Q // P
+E_TILES = E // P
+
+
+def tile_attend_passedthrough_written_lean_kernel(
+    tc, query, keys_words, keys_scales, factors, vals, old, fade, offs, offs2, offs3, offs4, out
+):
+    nc = tc.nc
+    with ExitStack() as ctx:
+        sb = ctx.enter_context(tc.tile_pool(name="sb", bufs=1))
+        ps = ctx.enter_context(tc.psum_pool(name="ps", bufs=1))
+
+        banks = [ps.tile([P, BANK], F32, name="bank%d" % b) for b in range(8)]
+        score_banks, sum_banks, val_banks, fade_banks = banks[0:2], banks[2:4], banks[4:6], banks[6:8]
+        read_banks = [fade_banks[0], fade_banks[1], score_banks[0]]
+
+        key_scales = sb.tile([P, T], U8, name="key_scales", align_bytes=64)
+        nc.gpsimd.memset(key_scales[:].bitcast(I32), 0)
+        fade_cols = sb.tile([P, M // BANK, PACK], F32, name="fade_cols")
+        nc.scalar.dma_start(out=fade_cols[:], in_=fade[0].rearrange("(h p c) -> p h c", p=P, c=PACK))
+        q_raw = sb.tile([P, PACK, Q], F32, name="q_raw")
+        nc.sync.dma_start(out=q_raw[:], in_=query.rearrange("(p t) q -> p t q", t=PACK))
+        for quad in range(4):
+            nc.sync.dma_start(
+                out=key_scales[32 * quad : 32 * quad + 4, :].bitcast(I32),
+                in_=keys_scales[0, 4 * quad : 4 * quad + 4, :].bitcast(I32),
+            )
+        tokens = sb.tile([P, I // 16], U16, name="tokens")
+        nc.sync.dma_start(tokens[:], offs)
+        key_words = sb.tile([P, T], U32, name="key_words", align_bytes=64)
+        nc.sync.dma_start(
+            out=key_words[:].bitcast(I32), in_=keys_words[0].rearrange("p n t -> p (n t)").bitcast(I32)
+        )
+        put_places = sb.tile([P, I // 16], U16, name="put_places")
+        get_places = sb.tile([P, I // 16], U16, name="get_places")
+        out_columns = sb.tile([P, Q // 16], U16, name="out_columns")
+        slot_factor = sb.tile([P, PACK], F32, name="slot_factor")
+        val_pool = [sb.tile([P, T], F32, name="val_pool%d" % e, tag="val_pool%d" % e, align_bytes=64) for e in range(E_TILES)]
+        old_rows = [sb.tile([P, M], F32, name="old_rows%d" % e) for e in range(E_TILES)]
+
+        def load_vals(e):
+            nc.sync.dma_start(out=val_pool[e][:], in_=vals[e * P : (e + 1) * P, :])
+
+        def load_old(e):
+            nc.sync.dma_start(out=old_rows[e][:], in_=old[e * P : (e + 1) * P, :])
+
+        nc.sync.dma_start(put_places[:], offs2)
+        load_old(0)
+        load_vals(0)
+        nc.sync.dma_start(get_places[:], offs3)
+        nc.sync.dma_start(out=slot_factor[:], in_=factors[0].rearrange("(p t) -> p t", t=PACK))
+        load_old(1)
+        load_old(2)
+        load_vals(1)
+        load_vals(2)
+        nc.sync.dma_start(out_columns[:], offs4)
+        load_vals(3)
+        load_old(3)
+
+        ident = sb.tile([P, P], F32, name="ident")
+        make_identity(nc, ident[:])
+
+        placed = [sb.tile([P, Z], F32, name="placed%d" % h) for h in range(Q_TILES)]
+        written = [sb.tile([P, M], F32, name="written%d" % e) for e in range(E_TILES)]
+
+        q_bf = sb.tile([P, Q, PACK], BF16, name="q_bf", align_bytes=64)
+        nc.scalar.copy(
+            out=q_bf[:].rearrange("p (c i) t -> p c t i", i=4),
+            in_=q_raw[:].rearrange("p t (c i) -> p c t i", i=4),
+        )
+        got_scales = sb.tile([P, I], U8, name="got_scales", align_bytes=64)
+        nc.vector.tensor_copy(got_scales[:], key_scales[:].indirect(tokens[:]))
+        q_codes = sb.tile([P, Q], U32, name="q_codes", align_bytes=64)
+        q_scales = sb.tile([P, Q], U8, name="q_scales", align_bytes=64)
+        nc.vector.quantize_mx(
+            out=q_codes[:].bitcast(FP8X4), scales=q_scales[:], in_=q_bf[:].rearrange("p q t -> p (q t)")
+        )
+        got_words = sb.tile([P, I], U32, name="got_words", align_bytes=64)
+        nc.vector.tensor_copy(got_words[:], key_words[:].indirect(tokens[:]))
+        for window in placed + written[:2]:
+            nc.vector.memset(window[:], 0.0)
+        for window in written[2:]:
+            nc.gpsimd.memset(window[:], 0.0)
+
+        fade_rows = sb.tile([P, M], F32, name="fade_rows")
+        for half in range(M // BANK):
+            bank = fade_banks[half][:].rearrange("e (c p) -> e c p", c=PACK)
+            for c in range(PACK):
+                nc.tensor.transpose(bank[:, c, :], fade_cols[:, half, c : c + 1].to_broadcast([P, P]), ident[:])
+            nc.scalar.copy(
+                out=fade_rows[:, half * BANK : (half + 1) * BANK].rearrange("e (p c) -> e p c", c=PACK),
+                in_=bank.rearrange("e c p -> e p c"),
+            )
+        kept = [sb.tile([P, M], F32, name="kept%d" % e) for e in range(E_TILES)]
+        for e in range(E_TILES):
+            nc.gpsimd.tensor_tensor(kept[e][:], old_rows[e][:], fade_rows[:], MULT)
+
+        def turn(bank, rows, first, last):
+            for t in range(PACK):
+                nc.tensor.matmul(
+                    bank[:, t * P : (t + 1) * P],
+                    lhsT=rows[:, t:I:PACK],
+                    rhs=ident[:],
+                    start=first and t == 0,
+                    stop=last and t == PACK - 1,
+                    is_transpose=True,
+                )
+
+        own = [sb.tile([P, I], F32, name="own%d" % h) for h in range(Q_TILES)]
+        passed = [sb.tile([P, I], F32, name="passed%d" % h) for h in range(Q_TILES)]
+        for h in range(Q_TILES):
+            rows = slice(h * P, (h + 1) * P)
+            nc.tensor.matmul_mx(
+                out=score_banks[h][:],
+                lhsT=q_codes[:, rows].bitcast(FP8X4),
+                lhsT_scale=q_scales[:, rows],
+                rhs=got_words[:].bitcast(FP8X4),
+                rhs_scale=got_scales[:],
+                start=True,
+                stop=True,
+            )
+        nc.vector.tensor_copy(own[0][:], score_banks[0][:])
+        nc.vector.tensor_copy(placed[0][:].indirect(put_places[:]), own[0][:])
+        nc.vector.tensor_copy(passed[0][:], placed[0][:].indirect(get_places[:]))
+        nc.scalar.copy(own[1][:], score_banks[1][:])
+        for part in range(2):
+            nc.scalar.activation(
+                placed[1][:].indirect(put_places[:, part * 16 : (part + 1) * 16]),
+                own[1][:, part * 256 : (part + 1) * 256],
+                COPY,
+            )
+        nc.scalar.activation(passed[1][:], placed[1][:].indirect(get_places[:]), COPY)
+        for h in range(Q_TILES):
+            turn(sum_banks[h], own[h], True, False)
+
+        def pick_values(pair, on_vector):
+            bank = val_banks[pair][:].rearrange("p (j u e) -> p j u e", j=2, u=2)
+            for j in range(2):
+                e = 2 * pair + j
+                got = sb.tile([P, I], BF16, name="got_vals%d" % e, align_bytes=64)
+                if on_vector:
+                    nc.vector.tensor_copy(got[:], val_pool[e][:].indirect(tokens[:]))
+                else:
+                    nc.scalar.activation(got[:], val_pool[e][:].indirect(tokens[:]), COPY)
+                pairs = got[:].bitcast(F32)
+                for u in range(2):
+                    nc.tensor.transpose(bank[:, j, u, :], pairs[:, u : I // 2 : 2], ident[:])
+
+        def quantise_values(pair, on_vector):
+            bank = val_banks[pair][:].rearrange("p (j u e) -> p j u e", j=2, u=2)
+            v_bf = sb.tile([P, 2 * P, PACK], BF16, name="v_bf%d" % pair, align_bytes=64)
+            words = v_bf[:].bitcast(F32).rearrange("p (j e) u -> p j e u", j=2)
+            if on_vector:
+                nc.vector.tensor_copy(out=words, in_=bank.rearrange("p j u e -> p j e u"))
+            else:
+                nc.scalar.copy(out=words, in_=bank.rearrange("p j u e -> p j e u"))
+            v_codes = sb.tile([P, 2 * P], U32, name="v_codes%d" % pair, align_bytes=64)
+            v_scales = sb.tile([P, 2 * P], U8, name="v_scales%d" % pair, align_bytes=64)
+            nc.vector.quantize_mx(
+                out=v_codes[:].bitcast(FP8X4), scales=v_scales[:], in_=v_bf[:].rearrange("p e t -> p (e t)")
+            )
+            return v_codes, v_scales
+
+        pick_values(0, True)
+        w_bf = sb.tile([P, Q, PACK], BF16, name="w_bf", tag="val_pool1", align_bytes=64)
+        for h in range(Q_TILES):
+            rows = slice(h * P, (h + 1) * P)
+            turn(sum_banks[h], passed[h], False, True)
+            weight = sb.tile([P, P, PACK], F32, name="weight%d" % h)
+            nc.scalar.activation(weight[:], sum_banks[h][:].rearrange("p (t q) -> p q t", t=PACK), SIGMOID)
+            nc.vector.tensor_tensor(
+                w_bf[:, rows, :], weight[:], slot_factor[:].unsqueeze(1).broadcast_to([P, P, PACK]), MULT
+            )
+        w_codes = sb.tile([P, Q], U32, name="w_codes", align_bytes=64)
+        w_scales = sb.tile([P, Q], U8, name="w_scales", align_bytes=64)
+        nc.vector.quantize_mx(
+            out=w_codes[:].bitcast(FP8X4), scales=w_scales[:], in_=w_bf[:].rearrange("p q t -> p (q t)")
+        )
+        v_quant = [quantise_values(0, True)]
+        pick_values(1, False)
+
+        def read_product(e, slot):
+            v_codes, v_scales = v_quant[e // 2]
+            cols = slice((e % 2) * P, (e % 2 + 1) * P)
+            nc.tensor.matmul_mx(
+                out=slot,
+                lhsT=v_codes[:, cols].bitcast(FP8X4),
+                lhsT_scale=v_scales[:, cols],
+                rhs=w_codes[:].bitcast(FP8X4),
+                rhs_scale=w_scales[:],
+                start=True,
+                stop=True,
+            )
+
+        def finish(e, result):
+            nc.vector.tensor_tensor(result[:], kept[e][:], written[e][:], ADD)
+            nc.sync.dma_start(out=out[e * P : (e + 1) * P, :], in_=result[:])
+
+        for e in range(2):
+            read_product(e, read_banks[0][:, e * Q : (e + 1) * Q])
+        read01 = sb.tile([P, 2 * Q], F32, name="read01", tag="val_pool3", align_bytes=64)
+        nc.vector.tensor_copy(read01[:], read_banks[0][:])
+        v_quant.append(quantise_values(1, False))
+        read_product(3, read_banks[2][:, 0:Q])
+        read_product(2, read_banks[1][:, 0:Q])
+        read3 = sb.tile([P, Q], F32, name="read3", tag="last")
+        nc.vector.tensor_copy(read3[:], read_banks[2][:, 0:Q])
+        read2 = sb.tile([P, Q], F32, name="read2")
+        nc.vector.tensor_copy(read2[:], read_banks[1][:, 0:Q])
+        nc.vector.tensor_copy(written[3][:].indirect(out_columns[:]), read3[:])
+        for e in range(2):
+            nc.scalar.activation(written[e][:].indirect(out_columns[:]), read01[:, e * Q : (e + 1) * Q], COPY)
+        nc.scalar.activation(written[2][:].indirect(out_columns[:]), read2[:], COPY)
+        result0 = sb.tile([P, M], F32, name="result0", tag="last")
+        finish(0, result0)
+        finish(3, kept[3])
+        finish(1, kept[1])
+        finish(2, kept[2])

@@ -35,7 +35,7 @@ def tile_attend_passedthrough_written_lean_kernel(
 
         banks = [ps.tile([P, BANK], F32, name="bank%d" % b) for b in range(8)]
         score_banks, sum_banks, val_banks, fade_banks = banks[0:2], banks[2:4], banks[4:6], banks[6:8]
-        read_banks = [fade_banks[0], fade_banks[1], score_banks[0]]
+        read_banks = fade_banks
 
         key_scales = sb.tile([P, T], U8, name="key_scales", align_bytes=64)
         nc.gpsimd.memset(key_scales[:].bitcast(I32), 0)
@@ -69,15 +69,15 @@ def tile_attend_passedthrough_written_lean_kernel(
 
         nc.sync.dma_start(put_places[:], offs2)
         load_old(0)
-        load_vals(0)
+        load_old(1)
         nc.sync.dma_start(get_places[:], offs3)
         nc.sync.dma_start(out=slot_factor[:], in_=factors[0].rearrange("(p t) -> p t", t=PACK))
-        load_old(1)
-        load_old(2)
+        load_vals(0)
         load_vals(1)
         load_vals(2)
         nc.sync.dma_start(out_columns[:], offs4)
         load_vals(3)
+        load_old(2)
         load_old(3)
 
         ident = sb.tile([P, P], F32, name="ident")
@@ -100,10 +100,8 @@ def tile_attend_passedthrough_written_lean_kernel(
         )
         got_words = sb.tile([P, I], U32, name="got_words", align_bytes=64)
         nc.vector.tensor_copy(got_words[:], key_words[:].indirect(tokens[:]))
-        for window in placed + written[:2]:
+        for window in placed + written:
             nc.vector.memset(window[:], 0.0)
-        for window in written[2:]:
-            nc.gpsimd.memset(window[:], 0.0)
 
         fade_rows = sb.tile([P, M], F32, name="fade_rows")
         for half in range(M // BANK):
@@ -115,8 +113,6 @@ def tile_attend_passedthrough_written_lean_kernel(
                 in_=bank.rearrange("e c p -> e p c"),
             )
         kept = [sb.tile([P, M], F32, name="kept%d" % e) for e in range(E_TILES)]
-        for e in range(E_TILES):
-            nc.gpsimd.tensor_tensor(kept[e][:], old_rows[e][:], fade_rows[:], MULT)
 
         def turn(bank, rows, first, last):
             for t in range(PACK):
@@ -215,27 +211,25 @@ def tile_attend_passedthrough_written_lean_kernel(
                 stop=True,
             )
 
-        def finish(e, result):
-            nc.vector.tensor_tensor(result[:], kept[e][:], written[e][:], ADD)
-            nc.sync.dma_start(out=out[e * P : (e + 1) * P, :], in_=result[:])
+        def finish(e, columns):
+            nc.vector.tensor_tensor(kept[e][:, columns], kept[e][:, columns], written[e][:, columns], ADD)
+            nc.sync.dma_start(out=out[e * P : (e + 1) * P, columns], in_=kept[e][:, columns])
 
         for e in range(2):
             read_product(e, read_banks[0][:, e * Q : (e + 1) * Q])
         read01 = sb.tile([P, 2 * Q], F32, name="read01", tag="val_pool3", align_bytes=64)
-        nc.vector.tensor_copy(read01[:], read_banks[0][:])
+        nc.scalar.copy(read01[:], read_banks[0][:])
         v_quant.append(quantise_values(1, False))
-        read_product(3, read_banks[2][:, 0:Q])
-        read_product(2, read_banks[1][:, 0:Q])
-        read3 = sb.tile([P, Q], F32, name="read3", tag="last")
-        nc.vector.tensor_copy(read3[:], read_banks[2][:, 0:Q])
-        read2 = sb.tile([P, Q], F32, name="read2")
-        nc.vector.tensor_copy(read2[:], read_banks[1][:, 0:Q])
-        nc.vector.tensor_copy(written[3][:].indirect(out_columns[:]), read3[:])
         for e in range(2):
-            nc.scalar.activation(written[e][:].indirect(out_columns[:]), read01[:, e * Q : (e + 1) * Q], COPY)
-        nc.scalar.activation(written[2][:].indirect(out_columns[:]), read2[:], COPY)
-        result0 = sb.tile([P, M], F32, name="result0", tag="last")
-        finish(0, result0)
-        finish(3, kept[3])
-        finish(1, kept[1])
-        finish(2, kept[2])
+            read_product(2 + e, read_banks[1][:, e * Q : (e + 1) * Q])
+        read23 = sb.tile([P, 2 * Q], F32, name="read23")
+        nc.vector.tensor_copy(read23[:], read_banks[1][:])
+        for e in range(E_TILES):
+            read = read01 if e < 2 else read23
+            nc.scalar.activation(written[e][:].indirect(out_columns[:]), read[:, (e % 2) * Q : (e % 2 + 1) * Q], COPY)
+        for e in range(E_TILES):
+            nc.vector.tensor_tensor(kept[e][:], old_rows[e][:], fade_rows[:], MULT)
+        for e in range(E_TILES - 1):
+            finish(e, slice(0, M))
+        for half in range(2):
+            finish(E_TILES - 1, slice(half * M // 2, (half + 1) * M // 2))

from contextlib import ExitStack

import concourse.mybir as mybir
from concourse.masks import make_identity

D, T, I, Q, E, Z, M = 512, 2048, 512, 256, 512, 1024, 1024
FLOPS = 2 * D * Q * I + 2 * I * E * Q

F32 = mybir.dt.float32
BF16 = mybir.dt.bfloat16
I32 = mybir.dt.int32
U32 = mybir.dt.uint32
U16 = mybir.dt.uint16
U8 = mybir.dt.uint8
FP8X4 = mybir.dt.float8_e4m3fn_x4
ADD = mybir.AluOpType.add
MULT = mybir.AluOpType.mult
COPY = mybir.ActivationFunctionType.Copy
SIGMOID = mybir.ActivationFunctionType.Sigmoid

P = 128
PACK = 4
BANK = 512
Q_TILES = Q // P
E_TILES = E // P


def tile_attend_passedthrough_written_lean_kernel(
    tc, query, keys_words, keys_scales, factors, vals, old, fade, offs, offs2, offs3, offs4, out
):
    nc = tc.nc
    with ExitStack() as ctx:
        sb = ctx.enter_context(tc.tile_pool(name="sb", bufs=1))
        ps = ctx.enter_context(tc.psum_pool(name="ps", bufs=1))

        banks = [ps.tile([P, BANK], F32, name="bank%d" % b) for b in range(8)]
        score_banks, sum_banks, val_banks, fade_banks = banks[0:2], banks[2:4], banks[4:6], banks[6:8]
        read_banks = fade_banks

        key_scales = sb.tile([P, T], U8, name="key_scales", align_bytes=64)
        nc.gpsimd.memset(key_scales[:].bitcast(I32), 0)
        fade_cols = sb.tile([P, M // BANK, PACK], F32, name="fade_cols")
        nc.scalar.dma_start(out=fade_cols[:], in_=fade[0].rearrange("(h p c) -> p h c", p=P, c=PACK))
        q_raw = sb.tile([P, PACK, Q], F32, name="q_raw")
        nc.sync.dma_start(out=q_raw[:], in_=query.rearrange("(p t) q -> p t q", t=PACK))
        for quad in range(4):
            nc.sync.dma_start(
                out=key_scales[32 * quad : 32 * quad + 4, :].bitcast(I32),
                in_=keys_scales[0, 4 * quad : 4 * quad + 4, :].bitcast(I32),
            )
        tokens = sb.tile([P, I // 16], U16, name="tokens")
        nc.sync.dma_start(tokens[:], offs)
        key_words = sb.tile([P, T], U32, name="key_words", align_bytes=64)
        nc.sync.dma_start(
            out=key_words[:].bitcast(I32), in_=keys_words[0].rearrange("p n t -> p (n t)").bitcast(I32)
        )
        put_places = sb.tile([P, I // 16], U16, name="put_places")
        get_places = sb.tile([P, I // 16], U16, name="get_places")
        out_columns = sb.tile([P, Q // 16], U16, name="out_columns")
        slot_factor = sb.tile([P, PACK], F32, name="slot_factor")
        val_pool = [sb.tile([P, T], F32, name="val_pool%d" % e, tag="val_pool%d" % e, align_bytes=64) for e in range(E_TILES)]
        old_rows = [sb.tile([P, M], F32, name="old_rows%d" % e) for e in range(E_TILES)]

        def load_vals(e):
            nc.sync.dma_start(out=val_pool[e][:], in_=vals[e * P : (e + 1) * P, :])

        def load_old(e):
            nc.sync.dma_start(out=old_rows[e][:], in_=old[e * P : (e + 1) * P, :])

        nc.sync.dma_start(put_places[:], offs2)
        load_old(0)
        load_old(1)
        nc.sync.dma_start(get_places[:], offs3)
        nc.sync.dma_start(out=slot_factor[:], in_=factors[0].rearrange("(p t) -> p t", t=PACK))
        load_vals(0)
        load_vals(1)
        load_vals(2)
        nc.sync.dma_start(out_columns[:], offs4)
        load_vals(3)
        load_old(2)
        load_old(3)

        ident = sb.tile([P, P], F32, name="ident")
        make_identity(nc, ident[:])

        placed = [sb.tile([P, Z], F32, name="placed%d" % h) for h in range(Q_TILES)]
        written = [sb.tile([P, M], F32, name="written%d" % e) for e in range(E_TILES)]

        q_bf = sb.tile([P, Q, PACK], BF16, name="q_bf", align_bytes=64)
        nc.scalar.copy(
            out=q_bf[:].rearrange("p (c i) t -> p c t i", i=4),
            in_=q_raw[:].rearrange("p t (c i) -> p c t i", i=4),
        )
        got_scales = sb.tile([P, I], U8, name="got_scales", align_bytes=64)
        nc.vector.tensor_copy(got_scales[:], key_scales[:].indirect(tokens[:]))
        q_codes = sb.tile([P, Q], U32, name="q_codes", align_bytes=64)
        q_scales = sb.tile([P, Q], U8, name="q_scales", align_bytes=64)
        nc.vector.quantize_mx(
            out=q_codes[:].bitcast(FP8X4), scales=q_scales[:], in_=q_bf[:].rearrange("p q t -> p (q t)")
        )
        got_words = sb.tile([P, I], U32, name="got_words", align_bytes=64)
        nc.vector.tensor_copy(got_words[:], key_words[:].indirect(tokens[:]))
        for window in placed + written:
            nc.vector.memset(window[:], 0.0)

        fade_rows = sb.tile([P, M], F32, name="fade_rows")
        for half in range(M // BANK):
            bank = fade_banks[half][:].rearrange("e (c p) -> e c p", c=PACK)
            for c in range(PACK):
                nc.tensor.transpose(bank[:, c, :], fade_cols[:, half, c : c + 1].to_broadcast([P, P]), ident[:])
            nc.scalar.copy(
                out=fade_rows[:, half * BANK : (half + 1) * BANK].rearrange("e (p c) -> e p c", c=PACK),
                in_=bank.rearrange("e c p -> e p c"),
            )
        kept = [sb.tile([P, M], F32, name="kept%d" % e) for e in range(E_TILES)]

        def turn(bank, rows, first, last):
            for t in range(PACK):
                nc.tensor.matmul(
                    bank[:, t * P : (t + 1) * P],
                    lhsT=rows[:, t:I:PACK],
                    rhs=ident[:],
                    start=first and t == 0,
                    stop=last and t == PACK - 1,
                    is_transpose=True,
                )

        own = [sb.tile([P, I], F32, name="own%d" % h) for h in range(Q_TILES)]
        passed = [sb.tile([P, I], F32, name="passed%d" % h) for h in range(Q_TILES)]
        for h in range(Q_TILES):
            rows = slice(h * P, (h + 1) * P)
            nc.tensor.matmul_mx(
                out=score_banks[h][:],
                lhsT=q_codes[:, rows].bitcast(FP8X4),
                lhsT_scale=q_scales[:, rows],
                rhs=got_words[:].bitcast(FP8X4),
                rhs_scale=got_scales[:],
                start=True,
                stop=True,
            )
        nc.vector.tensor_copy(own[0][:], score_banks[0][:])
        nc.vector.tensor_copy(placed[0][:].indirect(put_places[:]), own[0][:])
        nc.vector.tensor_copy(passed[0][:], placed[0][:].indirect(get_places[:]))
        nc.scalar.copy(own[1][:], score_banks[1][:])
        for part in range(2):
            nc.scalar.activation(
                placed[1][:].indirect(put_places[:, part * 16 : (part + 1) * 16]),
                own[1][:, part * 256 : (part + 1) * 256],
                COPY,
            )
        nc.scalar.activation(passed[1][:], placed[1][:].indirect(get_places[:]), COPY)
        for h in range(Q_TILES):
            turn(sum_banks[h], own[h], True, False)

        def pick_values(pair, on_vector):
            bank = val_banks[pair][:].rearrange("p (j u e) -> p j u e", j=2, u=2)
            for j in range(2):
                e = 2 * pair + j
                got = sb.tile([P, I], BF16, name="got_vals%d" % e, align_bytes=64)
                if on_vector:
                    nc.vector.tensor_copy(got[:], val_pool[e][:].indirect(tokens[:]))
                else:
                    nc.scalar.activation(got[:], val_pool[e][:].indirect(tokens[:]), COPY)
                pairs = got[:].bitcast(F32)
                for u in range(2):
                    nc.tensor.transpose(bank[:, j, u, :], pairs[:, u : I // 2 : 2], ident[:])

        def quantise_values(pair, on_vector):
            bank = val_banks[pair][:].rearrange("p (j u e) -> p j u e", j=2, u=2)
            v_bf = sb.tile([P, 2 * P, PACK], BF16, name="v_bf%d" % pair, align_bytes=64)
            words = v_bf[:].bitcast(F32).rearrange("p (j e) u -> p j e u", j=2)
            if on_vector:
                nc.vector.tensor_copy(out=words, in_=bank.rearrange("p j u e -> p j e u"))
            else:
                nc.scalar.copy(out=words, in_=bank.rearrange("p j u e -> p j e u"))
            v_codes = sb.tile([P, 2 * P], U32, name="v_codes%d" % pair, align_bytes=64)
            v_scales = sb.tile([P, 2 * P], U8, name="v_scales%d" % pair, align_bytes=64)
            nc.vector.quantize_mx(
                out=v_codes[:].bitcast(FP8X4), scales=v_scales[:], in_=v_bf[:].rearrange("p e t -> p (e t)")
            )
            return v_codes, v_scales

        pick_values(0, True)
        w_bf = sb.tile([P, Q, PACK], BF16, name="w_bf", tag="val_pool1", align_bytes=64)
        for h in range(Q_TILES):
            rows = slice(h * P, (h + 1) * P)
            turn(sum_banks[h], passed[h], False, True)
            weight = sb.tile([P, P, PACK], F32, name="weight%d" % h)
            nc.scalar.activation(weight[:], sum_banks[h][:].rearrange("p (t q) -> p q t", t=PACK), SIGMOID)
            nc.vector.tensor_tensor(
                w_bf[:, rows, :], weight[:], slot_factor[:].unsqueeze(1).broadcast_to([P, P, PACK]), MULT
            )
        w_codes = sb.tile([P, Q], U32, name="w_codes", align_bytes=64)
        w_scales = sb.tile([P, Q], U8, name="w_scales", align_bytes=64)
        nc.vector.quantize_mx(
            out=w_codes[:].bitcast(FP8X4), scales=w_scales[:], in_=w_bf[:].rearrange("p q t -> p (q t)")
        )
        v_quant = [quantise_values(0, True)]
        pick_values(1, False)

        def read_product(e, slot):
            v_codes, v_scales = v_quant[e // 2]
            cols = slice((e % 2) * P, (e % 2 + 1) * P)
            nc.tensor.matmul_mx(
                out=slot,
                lhsT=v_codes[:, cols].bitcast(FP8X4),
                lhsT_scale=v_scales[:, cols],
                rhs=w_codes[:].bitcast(FP8X4),
                rhs_scale=w_scales[:],
                start=True,
                stop=True,
            )

        def finish(e, columns):
            nc.vector.tensor_tensor(kept[e][:, columns], kept[e][:, columns], written[e][:, columns], ADD)
            nc.sync.dma_start(out=out[e * P : (e + 1) * P, columns], in_=kept[e][:, columns])

        for e in range(2):
            read_product(e, read_banks[0][:, e * Q : (e + 1) * Q])
        read01 = sb.tile([P, 2 * Q], F32, name="read01", tag="val_pool3", align_bytes=64)
        nc.scalar.copy(read01[:], read_banks[0][:])
        v_quant.append(quantise_values(1, False))
        for e in range(2):
            read_product(2 + e, read_banks[1][:, e * Q : (e + 1) * Q])
        read23 = sb.tile([P, 2 * Q], F32, name="read23")
        nc.vector.tensor_copy(read23[:], read_banks[1][:])
        for e in range(E_TILES):
            read = read01 if e < 2 else read23
            nc.scalar.activation(written[e][:].indirect(out_columns[:]), read[:, (e % 2) * Q : (e % 2 + 1) * Q], COPY)
        for e in range(E_TILES):
            nc.vector.tensor_tensor(kept[e][:], old_rows[e][:], fade_rows[:], MULT)
        for e in range(E_TILES - 1):
            finish(e, slice(0, M))
        for half in range(2):
            finish(E_TILES - 1, slice(half * M // 2, (half + 1) * M // 2))
